import numpy as np
import ml_dtypes


def mxq(x, axis, fmt="e4m3"):
    dtype, down = {"e4m3": (ml_dtypes.float8_e4m3fn, 7), "e5m2": (ml_dtypes.float8_e5m2, 14)}[fmt]
    v = np.moveaxis(np.asarray(x, np.float32).astype(ml_dtypes.bfloat16).astype(np.float64), axis, -1)
    blocks = v.reshape(v.shape[:-1] + (-1, 32))
    amax = np.abs(blocks).max(-1, keepdims=True)
    byte = np.maximum(np.where(amax > 0, np.frexp(amax)[1] - 1 + 127, 0) - down, 1)
    scale = np.exp2(byte - 127.0)
    codes = (blocks / scale).astype(np.float32).astype(dtype).astype(np.float64)
    return np.moveaxis((codes * scale).reshape(v.shape), -1, axis)


WIDE = False


def mx_kscale(k):
    if not WIDE:
        return np.ones(k)
    levels = np.array([10, -10, 5, -5, 0])
    if k % 512:
        return np.exp2(np.random.permutation(np.resize(levels, k // 32))).repeat(32)
    a = np.empty((k // 512, 16))
    for p in range(k // 512):
        a[p, :8] = np.random.permutation(np.resize(levels, 8))
        for g in range(8):
            far = levels[np.abs(levels - a[p, g]) >= 10]
            a[p, g + 8] = far[np.random.randint(len(far))]
    return np.exp2(a.ravel()).repeat(32)


def f64(x):
    return np.asarray(x).astype(np.float64)


def striped(idx):
    return np.tile(idx.reshape(-1, 16).T, (8, 1)).astype(np.uint16)


def unstriped(offs):
    return offs[:16].T.reshape(-1).astype(np.int64)


E2M1 = np.array([0.0, 0.5, 1.0, 1.5, 2.0, 3.0, 4.0, 6.0, -0.0, -0.5, -1.0, -1.5, -2.0, -3.0, -4.0, -6.0])


def pack_weight(w, fmt):
    k, n = w.shape
    w = f64(np.asarray(w, np.float32).astype(ml_dtypes.bfloat16)).reshape(k // 32, 32, n)
    amax = np.abs(w).max(1)
    if fmt == "e4m3":
        byte = np.frexp(amax)[1] - 1 + 127 - 7
    else:
        mant, ex = np.frexp(amax / 6.0)
        byte = np.where(mant > 0.5, ex, ex - 1) + 127
    byte = np.clip(np.where(amax > 0, byte, 1), 1, 254)
    scaled = (w * np.exp2(127.0 - byte)[:, None, :]).reshape(k, n).astype(np.float32)
    by_word = np.ascontiguousarray(scaled.reshape(k // 512, 128, 4, n).transpose(0, 1, 3, 2))
    if fmt == "e4m3":
        words = by_word.astype(ml_dtypes.float8_e4m3fn).view(np.uint8)
    else:
        c = by_word.astype(ml_dtypes.float4_e2m1fn).view(np.uint8) & 0xF
        words = (c[..., 0::2] | (c[..., 1::2] << 4)).reshape(k // 512, 128, 2 * n)
    return np.ascontiguousarray(words), np.ascontiguousarray(byte.astype(np.uint8).reshape(k // 512, 16, n))


def unpack_weight(words, scales, fmt):
    g, _, n = scales.shape
    words = np.ascontiguousarray(words).reshape(g, 128, n, -1)
    if fmt == "e4m3":
        vals = words.view(ml_dtypes.float8_e4m3fn).astype(np.float64)
    else:
        nib = np.empty((g, 128, n, 4), np.uint8)
        nib[..., 0::2] = words & 0xF
        nib[..., 1::2] = words >> 4
        vals = E2M1[nib]
    vals = vals * np.repeat(np.exp2(scales.astype(np.float64) - 127.0), 8, axis=1)[..., None]
    return vals.transpose(0, 1, 3, 2).reshape(g * 512, n)


def gelu(v):
    return 0.5 * v * (1.0 + np.tanh(np.sqrt(2.0 / np.pi) * (v + 0.044715 * v**3)))


K, T, S, S2 = 1024, 2048, 512, 1024

def setup_inputs():
    n = np.random.standard_normal
    s = mx_kscale(K)[:, None]
    d = {}
    d["tab_words"], d["tab_scales"] = pack_weight(n((K, T)) * s, "e4m3")
    d["offs"] = striped(np.random.permutation(T)[:S])
    d["offs2"] = striped(np.random.permutation(T)[:S2])
    d["w1"] = (n((K, K)) / s / s.T * (2.0 / K)).astype(np.float32)
    d["w2_words"], d["w2_scales"] = pack_weight(n((K, K)) / s / s.T * (2.0 / K), "e2m1")
    d["w3_words"], d["w3_scales"] = pack_weight(n((K, K)) / s / s.T * (2.0 / K), "e4m3")
    d["lean"] = n(S2).astype(np.float32)
    return d

def reference(tab_words, tab_scales, offs, offs2, w1, w2_words, w2_scales, w3_words, w3_scales, lean):
    TW = unpack_weight(tab_words, tab_scales, "e4m3")
    v = TW[:, unstriped(offs)]
    v2 = TW[:, unstriped(offs2)]
    w1q = mxq(f64(w1), 0, "e4m3")
    w2 = unpack_weight(w2_words, w2_scales, "e2m1")
    w3 = unpack_weight(w3_words, w3_scales, "e4m3")
    look = w1q.T @ v
    start = w2.T @ v
    end = w3.T @ v
    h = np.maximum(look, np.minimum(start, end))
    hq = mxq(h, 0, "e4m3")
    e = v2.T @ hq
    x = e + f64(lean)[:, None]
    out = 0.5 * x * (1.0 + np.tanh(0.7978845608028654 * (x + 0.044715 * x ** 3)))
    return out

@@ -1,0 +1,341 @@
+from contextlib import ExitStack
+
+import concourse.mybir as mybir
+from concourse.masks import make_identity
+
+K, T, S, S2 = 1024, 2048, 512, 1024
+FLOPS = 2 * K * K * S * 3 + 2 * K * S2 * S
+
+F32 = mybir.dt.float32
+BF16 = mybir.dt.bfloat16
+I32 = mybir.dt.int32
+U32 = mybir.dt.uint32
+U16 = mybir.dt.uint16
+U8 = mybir.dt.uint8
+FP8X4 = mybir.dt.float8_e4m3fn_x4
+FP4X4 = mybir.dt.float4_e2m1fn_x4
+ALU = mybir.AluOpType
+GELU = mybir.ActivationFunctionType.Gelu_apprx_tanh
+
+P = 128
+PACK = 4
+KP = P * PACK
+PASSES = K // KP
+HALF = 512
+JT = S // P
+JH = 256
+MT = S2 // P
+W1_CHUNKS = [(0, 0, 512), (1, 0, 512), (0, 512, 1024), (1, 512, 768), (1, 768, 1024)]
+SCALAR_COLS = [96, 192, 192, 144, 144]
+PIECES = [(0, 1), (2, 3)]
+TIES = {}
+LAST_ON_VECTOR = [(1, PIECES[-1])]
+GPSIMD_COLS = 128
+
+
+def tile_list_lookalike_name_screening_kernel(
+    tc, tab_words, tab_scales, offs, offs2, w1, w2_words, w2_scales, w3_words, w3_scales, lean, out
+):
+    nc = tc.nc
+    with ExitStack() as ctx:
+        keep = ctx.enter_context(tc.tile_pool(name="keep", bufs=1))
+        psum = ctx.enter_context(tc.psum_pool(name="psum", bufs=1))
+
+        def sb(name, shape, dtype, tag=""):
+            return keep.tile(shape, dtype, name=name, tag=tag, align_bytes=64)
+
+        def bank(n, shape):
+            return psum.tile(shape, F32, name="bank%d" % n)
+
+        idx = sb("idx", [P, S // 16], U16)
+        idx2 = sb("idx2", [P, S2 // 16], U16)
+        tab_planes = sb("tab_planes", [P, T], U8)
+        v_plane1 = sb("v_plane1", [P, S], U8)
+        ident = sb("ident", [P, P], F32)
+
+        nc.vector.memset(tab_planes[:].bitcast(I32), 0)
+        with tc.tile_pool(name="early", bufs=1) as early:
+            zeros = early.tile([P, S // 4], I32, name="zeros")
+            nc.gpsimd.memset(zeros[:], 0)
+            nc.vector.tensor_copy(v_plane1[:].bitcast(I32), zeros[:])
+        warm = sb("warm", [P, 1], F32)
+        warm_out = sb("warm_out", [P, 1], F32)
+        nc.gpsimd.memset(warm[:], 0.0)
+        nc.scalar.activation(warm_out[:], warm[:], GELU)
+        late = ctx.enter_context(tc.tile_pool(name="late", bufs=1))
+
+        def landing(name, shape, dtype, tag=""):
+            return late.tile(shape, dtype, name=name, tag=TIES.get(name, tag), align_bytes=64)
+
+        w2_planes = landing("w2_planes", [P, PASSES * K], U8)
+        w3_planes = landing("w3_planes", [P, K], U8)
+        nc.vector.memset(w3_planes[:].bitcast(I32), 0)
+        nc.vector.memset(w2_planes[:].bitcast(I32), 0)
+        tab = [landing("tab%d" % a, [P, T], U32) for a in range(PASSES)]
+        nc.sync.dma_start(idx[:], offs)
+        nc.sync.dma_start(idx2[:], offs2)
+
+        def load_tab(a):
+            nc.sync.dma_start(tab[a][:].bitcast(I32), tab_words[a].rearrange("p t i -> p (t i)").bitcast(I32))
+
+        make_identity(nc, ident[:])
+
+        w3c = {}
+
+        def load_w3(a, alloc):
+            w3c[a] = alloc("w3c%d" % a, [P, K], U32)
+            nc.sync.dma_start(w3c[a][:].bitcast(I32), w3_words[a].rearrange("p c i -> p (c i)").bitcast(I32))
+
+        w1_raw = {}
+
+        def load_w1(chunk):
+            a, c0, c1 = chunk
+            w1_raw[chunk] = landing("w1_raw%d_%d" % (a, c0), [P, PACK, c1 - c0], F32)
+            nc.sync.dma_start(
+                w1_raw[chunk][:], w1[KP * a : KP * (a + 1), c0:c1].rearrange("(p i) r -> p i r", i=PACK)
+            )
+
+        v_words = {(a, h): sb("v_words%d%d" % (a, h), [P, S // 2], U32) for a in range(PASSES) for h in range(2)}
+        v2_words = {}
+        v_planes = sb("v_planes", [P, S], U8)
+        v2_planes = {}
+
+        def gather(dst, window, offsets):
+            nc.vector.tensor_copy(dst[:], window[:].indirect(offsets[:]))
+
+        def gather_v2_planes(half, tag=""):
+            v2_planes[half] = sb("v2_planes%d" % half, [P, S2 // 2], U8, tag)
+            gather(v2_planes[half], tab_planes, idx2[:, 32 * half : 32 * (half + 1)])
+
+        def gather_v2_words(a, m0, m1):
+            piece = landing("v2_words%d_%d" % (a, m0), [P, (m1 - m0) * P], U32)
+            for mt in range(m0, m1):
+                v2_words[a, mt] = piece[:, (mt - m0) * P : (mt - m0 + 1) * P]
+            gather(piece, tab[a], idx2[:, 8 * m0 : 8 * m1])
+
+        load_w3(0, sb)
+        for q in range(4):
+            nc.sync.dma_start(
+                tab_planes[32 * q : 32 * q + 8, :].bitcast(I32), tab_scales[:, 4 * q : 4 * q + 4, :].bitcast(I32)
+            )
+        load_tab(0)
+        for q in range(4):
+            nc.sync.dma_start(
+                w3_planes[32 * q : 32 * q + 8, :].bitcast(I32), w3_scales[:, 4 * q : 4 * q + 4, :].bitcast(I32)
+            )
+        load_tab(1)
+        load_w3(1, landing)
+        gather(v_planes, tab_planes, idx)
+        nc.sync.dma_start(v_plane1[0 : P - 4, :].bitcast(I32), v_planes[4:P, :].bitcast(I32))
+        for q in range(4):
+            nc.sync.dma_start(
+                w2_planes[32 * q : 32 * q + 4, :].bitcast(I32).rearrange("r (a c) -> r a c", a=PASSES),
+                w2_scales[:, 4 * q : 4 * q + 4, :].bitcast(I32).rearrange("a r c -> r a c"),
+            )
+        w2c = landing("w2c", [P, PASSES * 2 * K], U8)
+        nc.sync.dma_start(
+            w2c[:].bitcast(I32).rearrange("p (a c) -> p a c", a=PASSES), w2_words.bitcast(I32).rearrange("a p c -> p a c")
+        )
+        for chunk in W1_CHUNKS:
+            load_w1(chunk)
+        lean_col = landing("lean_col", [P, MT], F32)
+        with nc.allow_non_contiguous_dma(reason="one offset for each partition and tile of approved names"):
+            nc.sync.dma_start(lean_col[:], lean.rearrange("(t p) -> p t", p=P))
+
+        for h in range(2):
+            gather(v_words[0, h], tab[0], idx[:, 16 * h : 16 * (h + 1)])
+        gather_v2_planes(0)
+        gather_v2_words(0, 0, 4)
+        for h in range(2):
+            gather(v_words[1, h], tab[1], idx[:, 16 * h : 16 * (h + 1)])
+        gather_v2_words(1, 0, 4)
+
+        def v_operand(a, jt, at_zero=False):
+            cols = slice(jt * P, (jt + 1) * P)
+            plane = v_plane1[:, cols] if at_zero and a == 1 else v_planes[4 * a : P, cols]
+            return dict(lhsT=v_words[a, jt // 2][:, jt % 2 * P : (jt % 2 + 1) * P].bitcast(FP8X4), lhsT_scale=plane)
+
+        def w2_pass(acc, rh, a, jt):
+            nc.tensor.matmul_mx(
+                out=acc[:],
+                rhs=w2c[:, 2 * (K * a + HALF * rh) : 2 * (K * a + HALF * (rh + 1))].bitcast(FP4X4),
+                rhs_scale=w2_planes[:, K * a + HALF * rh : K * a + HALF * (rh + 1)],
+                start=(a == 0),
+                stop=(a == PASSES - 1),
+                **v_operand(a, jt, True),
+            )
+
+        def w3_pass(acc, rh, a, jt):
+            nc.tensor.matmul_mx(
+                out=acc[:],
+                rhs=w3c[a][:, HALF * rh : HALF * (rh + 1)].bitcast(FP8X4),
+                rhs_scale=w3_planes[4 * a : P, HALF * rh : HALF * (rh + 1)],
+                start=(a == 0),
+                stop=(a == PASSES - 1),
+                **v_operand(a, jt),
+            )
+
+        w1_grouped = {}
+        w1_codes = {}
+        w1_plane = {}
+
+        def cast_w1(chunk):
+            a, c0, c1 = chunk
+            grouped = landing("w1_grouped%d_%d" % (a, c0), [P, c1 - c0, PACK], BF16)
+            w1_grouped[chunk] = grouped
+            raw = w1_raw[chunk]
+            share = SCALAR_COLS[W1_CHUNKS.index(chunk)]
+            if share:
+                nc.scalar.copy(
+                    grouped[:, :share, :].rearrange("p (c i) t -> p c t i", i=4),
+                    raw[:, :, :share].rearrange("p t (c i) -> p c t i", i=4),
+                )
+            for g0 in range(share, c1 - c0, GPSIMD_COLS):
+                g1 = min(g0 + GPSIMD_COLS, c1 - c0)
+                nc.gpsimd.tensor_scalar(
+                    grouped[:, g0:g1, :], raw[:, :, g0:g1].rearrange("p t c -> p c t"), 1.0, 0.0, ALU.mult, ALU.add
+                )
+
+        def quantize_w1(chunk):
+            a, c0, c1 = chunk
+            w1_codes[chunk] = landing("w1_codes%d_%d" % (a, c0), [P, c1 - c0], U32)
+            w1_plane[chunk] = landing("w1_plane%d_%d" % (a, c0), [P, c1 - c0], U8)
+            nc.vector.quantize_mx(
+                out=w1_codes[chunk][:].bitcast(FP8X4),
+                scales=w1_plane[chunk][:],
+                in_=w1_grouped[chunk][:].rearrange("p c t -> p (c t)"),
+            )
+
+        def w1_pass(acc, chunk, jt):
+            a, c0, c1 = chunk
+            nc.tensor.matmul_mx(
+                out=acc[:, c0 % HALF : (c1 - 1) % HALF + 1],
+                rhs=w1_codes[chunk][:].bitcast(FP8X4),
+                rhs_scale=w1_plane[chunk][:],
+                start=(a == 0),
+                stop=(a == PASSES - 1 and c1 % HALF == 0),
+                **v_operand(a, jt),
+            )
+
+        def dealt(acc):
+            return acc[:].rearrange("j (p u e) -> j u p e", u=2, e=2)
+
+        def as_dealt(tile):
+            return tile[:].rearrange("j (u p e) -> j u p e", u=2, e=2)
+
+        smaller = {}
+
+        units = [(rh, jt) for rh in range(2) for jt in range(JT)]
+
+        def unit_bank(rh, jt):
+            return bank(JT * rh + jt, [P, HALF])
+
+        end_acc = {unit: unit_bank(*unit) for unit in units}
+        end_sb = {}
+        for jt in range(JT):
+            for rh in range(2):
+                w3_pass(end_acc[rh, jt], rh, 0, jt)
+        for rh, jt in units:
+            w3_pass(end_acc[rh, jt], rh, 1, jt)
+        gather_v2_planes(1, "w3c0")
+        gather_v2_words(0, 4, 8)
+        gather_v2_words(1, 4, 8)
+        for rh, jt in units:
+            end_sb[rh, jt] = landing("end_sb%d%d" % (rh, jt), [P, HALF], F32)
+            nc.scalar.copy(as_dealt(end_sb[rh, jt]), dealt(end_acc[rh, jt]))
+        for n, (rh, jt) in enumerate(units):
+            if n in (4, 6):
+                chunk = W1_CHUNKS[(4, 6).index(n)]
+                cast_w1(chunk)
+                quantize_w1(chunk)
+            start_acc = unit_bank(rh, jt)
+            for a in range(PASSES):
+                w2_pass(start_acc, rh, a, jt)
+            smaller[rh, jt] = landing("smaller%d%d" % (rh, jt), [P, HALF], F32)
+            nc.vector.tensor_tensor(as_dealt(smaller[rh, jt]), dealt(start_acc), as_dealt(end_sb[rh, jt]), ALU.min)
+
+        h_rows = {}
+
+        def take_max(rh, jt):
+            h_rows[rh, jt] = landing("h_rows%d%d" % (rh, jt), [P, HALF], BF16)
+            nc.vector.tensor_tensor(as_dealt(h_rows[rh, jt]), dealt(look[rh, jt]), as_dealt(smaller[rh, jt]), ALU.max)
+
+        h_grouped = {}
+        h_codes = {}
+        h_plane = {}
+
+        def turn(rh, piece):
+            turned = bank(JT * rh + piece[0], [P, len(piece), 2, P])
+            for t, jt in enumerate(piece):
+                words = h_rows[rh, jt][:].bitcast(F32)
+                for u in range(2):
+                    nc.tensor.transpose(turned[:, t, u, :], words[:, u * P : (u + 1) * P], ident[:])
+            h_grouped[rh, piece] = landing("h_grouped%d%d" % (rh, piece[0]), [P, len(piece) * P * PACK], BF16)
+            copy_out = nc.vector.tensor_copy if (rh, piece) in LAST_ON_VECTOR else nc.scalar.copy
+            copy_out(
+                h_grouped[rh, piece][:].bitcast(F32).rearrange("p (t j u) -> p t j u", t=len(piece), u=2),
+                turned[:].rearrange("p t u j -> p t j u"),
+            )
+
+        def quantize_h(rh, piece):
+            h_codes[rh, piece] = landing("h_codes%d%d" % (rh, piece[0]), [P, len(piece) * P], U32)
+            h_plane[rh, piece] = landing("h_plane%d%d" % (rh, piece[0]), [P, len(piece) * P], U8)
+            nc.vector.quantize_mx(
+                out=h_codes[rh, piece][:].bitcast(FP8X4), scales=h_plane[rh, piece][:], in_=h_grouped[rh, piece][:]
+            )
+
+        def match_pass(acc, tiles, b, piece):
+            for t, mt in enumerate(tiles):
+                nc.tensor.matmul_mx(
+                    out=acc[:, t, :],
+                    lhsT=v2_words[b, mt].bitcast(FP8X4),
+                    lhsT_scale=v2_planes[mt // 4][4 * b : P, mt % 4 * P : (mt % 4 + 1) * P],
+                    rhs=h_codes[b, piece][:].bitcast(FP8X4),
+                    rhs_scale=h_plane[b, piece][:],
+                    start=(b == 0 and t == 0),
+                    stop=(b == PASSES - 1 and t == len(tiles) - 1),
+                )
+
+        def finish(acc, tiles, piece):
+            res = landing("res%d%d" % (tiles[0], piece[0]), [P, len(tiles), len(piece) * P], F32)
+            for t, mt in enumerate(tiles):
+                nc.scalar.activation(res[:, t, :], acc[:, t, :], GELU, bias=lean_col[:, mt : mt + 1])
+            nc.sync.dma_start(
+                out[tiles[0] * P : (tiles[-1] + 1) * P, piece[0] * P : (piece[-1] + 1) * P].rearrange(
+                    "(t p) j -> p t j", p=P
+                ),
+                res[:],
+            )
+
+        def look_passes(chunks, tiles):
+            for chunk in chunks:
+                for jt in tiles:
+                    w1_pass(look[chunk[1] // HALF, jt], chunk, jt)
+
+        def open_match(piece, banks, m0=0):
+            per_bank = JT // len(piece)
+            return [(bank(n, [P, per_bank, len(piece) * P]), tuple(range(m0 + i * per_bank, m0 + (i + 1) * per_bank))) for i, n in enumerate(banks)]
+
+        look = {unit: unit_bank(*unit) for unit in units}
+        for chunk in W1_CHUNKS[2:]:
+            cast_w1(chunk)
+            quantize_w1(chunk)
+        look_passes(W1_CHUNKS[:3], range(JT))
+        for piece in PIECES:
+            look_passes(W1_CHUNKS[3:], piece)
+        for n, piece in enumerate(PIECES):
+            for rh in range(2):
+                for jt in piece:
+                    take_max(rh, jt)
+                turn(rh, piece)
+            for rh in range(2):
+                quantize_h(rh, piece)
+            if n == 0:
+                pass
+        for piece in PIECES:
+            match = open_match(piece, [JT * rh + jt for jt in reversed(piece) for rh in range(2)])
+            for acc, tiles in match:
+                match_pass(acc, tiles, 0, piece)
+            for acc, tiles in match:
+                match_pass(acc, tiles, 1, piece)
+                finish(acc, tiles, piece)

@@ -26,7 +26,7 @@ JT = S // P
 JH = 256
 MT = S2 // P
 W1_CHUNKS = [(0, 0, 512), (1, 0, 512), (0, 512, 1024), (1, 512, 768), (1, 768, 1024)]
-SCALAR_COLS = [96, 192, 192, 144, 144]
+SCALAR_COLS = [512, 384, 384, 128, 128]
 PIECES = [(0, 1), (2, 3)]
 TIES = {}
 LAST_ON_VECTOR = [(1, PIECES[-1])]
@@ -68,7 +68,7 @@ def tile_list_lookalike_name_screening_kernel(
             return late.tile(shape, dtype, name=name, tag=TIES.get(name, tag), align_bytes=64)
 
         w2_planes = landing("w2_planes", [P, PASSES * K], U8)
-        w3_planes = landing("w3_planes", [P, K], U8)
+        w3_planes = landing("w3_planes", [P, PASSES * K], U8)
         nc.vector.memset(w3_planes[:].bitcast(I32), 0)
         nc.vector.memset(w2_planes[:].bitcast(I32), 0)
         tab = [landing("tab%d" % a, [P, T], U32) for a in range(PASSES)]
@@ -78,7 +78,6 @@ def tile_list_lookalike_name_screening_kernel(
         def load_tab(a):
             nc.sync.dma_start(tab[a][:].bitcast(I32), tab_words[a].rearrange("p t i -> p (t i)").bitcast(I32))
 
-        make_identity(nc, ident[:])
 
         w3c = {}
 
@@ -88,9 +87,9 @@ def tile_list_lookalike_name_screening_kernel(
 
         w1_raw = {}
 
-        def load_w1(chunk):
+        def load_w1(chunk, alloc=landing):
             a, c0, c1 = chunk
-            w1_raw[chunk] = landing("w1_raw%d_%d" % (a, c0), [P, PACK, c1 - c0], F32)
+            w1_raw[chunk] = alloc("w1_raw%d_%d" % (a, c0), [P, PACK, c1 - c0], F32)
             nc.sync.dma_start(
                 w1_raw[chunk][:], w1[KP * a : KP * (a + 1), c0:c1].rearrange("(p i) r -> p i r", i=PACK)
             )
@@ -104,7 +103,7 @@ def tile_list_lookalike_name_screening_kernel(
             nc.vector.tensor_copy(dst[:], window[:].indirect(offsets[:]))
 
         def gather_v2_planes(half, tag=""):
-            v2_planes[half] = sb("v2_planes%d" % half, [P, S2 // 2], U8, tag)
+            v2_planes[half] = landing("v2_planes%d" % half, [P, S2 // 2], U8, tag)
             gather(v2_planes[half], tab_planes, idx2[:, 32 * half : 32 * (half + 1)])
 
         def gather_v2_words(a, m0, m1):
@@ -113,31 +112,49 @@ def tile_list_lookalike_name_screening_kernel(
                 v2_words[a, mt] = piece[:, (mt - m0) * P : (mt - m0 + 1) * P]
             gather(piece, tab[a], idx2[:, 8 * m0 : 8 * m1])
 
+        def load_planes(queue, planes, scales):
+            for q in range(4):
+                queue.dma_start(
+                    planes[32 * q : 32 * q + 4, :].bitcast(I32).rearrange("r (a c) -> r a c", a=PASSES),
+                    scales[:, 4 * q : 4 * q + 4, :].bitcast(I32).rearrange("a r c -> r a c"),
+                )
+
+        def load_tab_planes():
+            for q in range(4):
+                nc.sync.dma_start(
+                    tab_planes[32 * q : 32 * q + 8, :].bitcast(I32), tab_scales[:, 4 * q : 4 * q + 4, :].bitcast(I32)
+                )
+
+        def shift_plane():
+            gather(v_planes, tab_planes, idx)
+            for q in range(4):
+                nc.sync.dma_start(
+                    v_plane1[32 * q : 32 * q + 4, :].bitcast(I32), v_planes[32 * q + 4 : 32 * q + 8, :].bitcast(I32)
+                )
+
+        w2c = landing("w2c", [P, PASSES * 2 * K], U8)
+
+        def load_w2():
+            nc.sync.dma_start(
+                w2c[:].bitcast(I32).rearrange("p (a c) -> p a c", a=PASSES),
+                w2_words.bitcast(I32).rearrange("a p c -> p a c"),
+            )
+
+        load_planes(nc.gpsimd, w2_planes, w2_scales)
+        make_identity(nc, ident[:])
         load_w3(0, sb)
-        for q in range(4):
-            nc.sync.dma_start(
-                tab_planes[32 * q : 32 * q + 8, :].bitcast(I32), tab_scales[:, 4 * q : 4 * q + 4, :].bitcast(I32)
-            )
+        load_tab_planes()
         load_tab(0)
-        for q in range(4):
-            nc.sync.dma_start(
-                w3_planes[32 * q : 32 * q + 8, :].bitcast(I32), w3_scales[:, 4 * q : 4 * q + 4, :].bitcast(I32)
-            )
+        load_planes(nc.sync, w3_planes, w3_scales)
+        load_w1(W1_CHUNKS[0])
         load_tab(1)
         load_w3(1, landing)
-        gather(v_planes, tab_planes, idx)
-        nc.sync.dma_start(v_plane1[0 : P - 4, :].bitcast(I32), v_planes[4:P, :].bitcast(I32))
-        for q in range(4):
-            nc.sync.dma_start(
-                w2_planes[32 * q : 32 * q + 4, :].bitcast(I32).rearrange("r (a c) -> r a c", a=PASSES),
-                w2_scales[:, 4 * q : 4 * q + 4, :].bitcast(I32).rearrange("a r c -> r a c"),
-            )
-        w2c = landing("w2c", [P, PASSES * 2 * K], U8)
-        nc.sync.dma_start(
-            w2c[:].bitcast(I32).rearrange("p (a c) -> p a c", a=PASSES), w2_words.bitcast(I32).rearrange("a p c -> p a c")
-        )
-        for chunk in W1_CHUNKS:
-            load_w1(chunk)
+        shift_plane()
+        load_w2()
+        load_w1(W1_CHUNKS[1])
+        load_w1(W1_CHUNKS[2])
+        load_w1(W1_CHUNKS[3])
+        load_w1(W1_CHUNKS[4])
         lean_col = landing("lean_col", [P, MT], F32)
         with nc.allow_non_contiguous_dma(reason="one offset for each partition and tile of approved names"):
             nc.sync.dma_start(lean_col[:], lean.rearrange("(t p) -> p t", p=P))
@@ -169,7 +186,7 @@ def tile_list_lookalike_name_screening_kernel(
             nc.tensor.matmul_mx(
                 out=acc[:],
                 rhs=w3c[a][:, HALF * rh : HALF * (rh + 1)].bitcast(FP8X4),
-                rhs_scale=w3_planes[4 * a : P, HALF * rh : HALF * (rh + 1)],
+                rhs_scale=w3_planes[:, K * a + HALF * rh : K * a + HALF * (rh + 1)],
                 start=(a == 0),
                 stop=(a == PASSES - 1),
                 **v_operand(a, jt),
@@ -190,10 +207,10 @@ def tile_list_lookalike_name_screening_kernel(
                     grouped[:, :share, :].rearrange("p (c i) t -> p c t i", i=4),
                     raw[:, :, :share].rearrange("p t (c i) -> p c t i", i=4),
                 )
-            for g0 in range(share, c1 - c0, GPSIMD_COLS):
-                g1 = min(g0 + GPSIMD_COLS, c1 - c0)
-                nc.gpsimd.tensor_scalar(
-                    grouped[:, g0:g1, :], raw[:, :, g0:g1].rearrange("p t c -> p c t"), 1.0, 0.0, ALU.mult, ALU.add
+            if share < c1 - c0:
+                nc.vector.tensor_copy(
+                    grouped[:, share:, :].rearrange("p (c i) t -> p c t i", i=4),
+                    raw[:, :, share:].rearrange("p t (c i) -> p c t i", i=4),
                 )
 
         def quantize_w1(chunk):
@@ -225,7 +242,7 @@ def tile_list_lookalike_name_screening_kernel(
 
         smaller = {}
 
-        units = [(rh, jt) for rh in range(2) for jt in range(JT)]
+        units = [(rh, jt) for jt in range(JT) for rh in range(2)]
 
         def unit_bank(rh, jt):
             return bank(JT * rh + jt, [P, HALF])
@@ -237,22 +254,24 @@ def tile_list_lookalike_name_screening_kernel(
                 w3_pass(end_acc[rh, jt], rh, 0, jt)
         for rh, jt in units:
             w3_pass(end_acc[rh, jt], rh, 1, jt)
-        gather_v2_planes(1, "w3c0")
+        gather_v2_planes(1, "w3c1")
         gather_v2_words(0, 4, 8)
         gather_v2_words(1, 4, 8)
         for rh, jt in units:
             end_sb[rh, jt] = landing("end_sb%d%d" % (rh, jt), [P, HALF], F32)
             nc.scalar.copy(as_dealt(end_sb[rh, jt]), dealt(end_acc[rh, jt]))
-        for n, (rh, jt) in enumerate(units):
-            if n in (4, 6):
-                chunk = W1_CHUNKS[(4, 6).index(n)]
-                cast_w1(chunk)
-                quantize_w1(chunk)
-            start_acc = unit_bank(rh, jt)
+        start_acc = {}
+
+        def start_product(rh, jt):
+            start_acc[rh, jt] = unit_bank(rh, jt)
             for a in range(PASSES):
-                w2_pass(start_acc, rh, a, jt)
+                w2_pass(start_acc[rh, jt], rh, a, jt)
+
+        def take_min(rh, jt):
             smaller[rh, jt] = landing("smaller%d%d" % (rh, jt), [P, HALF], F32)
-            nc.vector.tensor_tensor(as_dealt(smaller[rh, jt]), dealt(start_acc), as_dealt(end_sb[rh, jt]), ALU.min)
+            nc.vector.tensor_tensor(
+                as_dealt(smaller[rh, jt]), dealt(start_acc[rh, jt]), as_dealt(end_sb[rh, jt]), ALU.min
+            )
 
         h_rows = {}
 
@@ -316,22 +335,25 @@ def tile_list_lookalike_name_screening_kernel(
             per_bank = JT // len(piece)
             return [(bank(n, [P, per_bank, len(piece) * P]), tuple(range(m0 + i * per_bank, m0 + (i + 1) * per_bank))) for i, n in enumerate(banks)]
 
-        look = {unit: unit_bank(*unit) for unit in units}
-        for chunk in W1_CHUNKS[2:]:
-            cast_w1(chunk)
-            quantize_w1(chunk)
-        look_passes(W1_CHUNKS[:3], range(JT))
-        for piece in PIECES:
-            look_passes(W1_CHUNKS[3:], piece)
+        look = {}
+        for rh, jt in units:
+            start_product(rh, jt)
         for n, piece in enumerate(PIECES):
+            for jt in piece:
+                for rh in range(2):
+                    take_min(rh, jt)
+                    look[rh, jt] = unit_bank(rh, jt)
+            if n == 0:
+                for chunk in W1_CHUNKS:
+                    cast_w1(chunk)
+                    quantize_w1(chunk)
+            look_passes(W1_CHUNKS, piece)
             for rh in range(2):
                 for jt in piece:
                     take_max(rh, jt)
                 turn(rh, piece)
             for rh in range(2):
                 quantize_h(rh, piece)
-            if n == 0:
-                pass
         for piece in PIECES:
             match = open_match(piece, [JT * rh + jt for jt in reversed(piece) for rh in range(2)])
             for acc, tiles in match:

@@ -19,18 +19,17 @@ GELU = mybir.ActivationFunctionType.Gelu_apprx_tanh
 
 P = 128
 PACK = 4
-KP = P * PACK
-PASSES = K // KP
-HALF = 512
-JT = S // P
-JH = 256
-MT = S2 // P
-W1_CHUNKS = [(0, 0, 512), (1, 0, 512), (0, 512, 1024), (1, 512, 768), (1, 768, 1024)]
-SCALAR_COLS = [512, 384, 384, 128, 128]
-PIECES = [(0, 1), (2, 3)]
-TIES = {}
-LAST_ON_VECTOR = [(1, PIECES[-1])]
-GPSIMD_COLS = 128
+PASS = P * PACK
+PASSES = K // PASS
+QUADRANTS = 4
+ROWS = 4
+PER_COLUMN = 16
+J_TILES = S // P
+J_HALVES = ((0, 1), (2, 3))
+J_HALF = 2 * P
+M_TILES = S2 // P
+
+W1_CHUNKS = ((0, 0, 512, 512), (1, 0, 512, 512), (0, 512, 1024, 448), (1, 512, 768, 128), (1, 768, 1024, 128))
 
 
 def tile_list_lookalike_name_screening_kernel(
@@ -41,323 +40,247 @@ def tile_list_lookalike_name_screening_kernel(
         keep = ctx.enter_context(tc.tile_pool(name="keep", bufs=1))
         psum = ctx.enter_context(tc.psum_pool(name="psum", bufs=1))
 
-        def sb(name, shape, dtype, tag=""):
-            return keep.tile(shape, dtype, name=name, tag=tag, align_bytes=64)
+        def kept(name, shape, dtype):
+            return keep.tile(shape, dtype, name=name, align_bytes=64)
 
-        def bank(n, shape):
-            return psum.tile(shape, F32, name="bank%d" % n)
+        def bank(rh, jt, shape):
+            return psum.tile(shape, F32, name="bank%d%d" % (rh, jt))
 
-        idx = sb("idx", [P, S // 16], U16)
-        idx2 = sb("idx2", [P, S2 // 16], U16)
-        tab_planes = sb("tab_planes", [P, T], U8)
-        v_plane1 = sb("v_plane1", [P, S], U8)
-        ident = sb("ident", [P, P], F32)
+        idx = kept("idx", [P, S // PER_COLUMN], U16)
+        idx2 = kept("idx2", [P, S2 // PER_COLUMN], U16)
+        tab_planes = kept("tab_planes", [P, T], U8)
+        v_plane1 = kept("v_plane1", [P, S], U8)
+        w3_codes = [kept("w3_codes0", [P, K], U32)]
 
         nc.vector.memset(tab_planes[:].bitcast(I32), 0)
         with tc.tile_pool(name="early", bufs=1) as early:
             zeros = early.tile([P, S // 4], I32, name="zeros")
             nc.gpsimd.memset(zeros[:], 0)
             nc.vector.tensor_copy(v_plane1[:].bitcast(I32), zeros[:])
-        warm = sb("warm", [P, 1], F32)
-        warm_out = sb("warm_out", [P, 1], F32)
+        warm = kept("warm", [P, 1], F32)
+        warm_out = kept("warm_out", [P, 1], F32)
         nc.gpsimd.memset(warm[:], 0.0)
         nc.scalar.activation(warm_out[:], warm[:], GELU)
         late = ctx.enter_context(tc.tile_pool(name="late", bufs=1))
 
-        def landing(name, shape, dtype, tag=""):
-            return late.tile(shape, dtype, name=name, tag=TIES.get(name, tag), align_bytes=64)
+        def tile(name, shape, dtype):
+            return late.tile(shape, dtype, name=name, align_bytes=64)
 
-        w2_planes = landing("w2_planes", [P, PASSES * K], U8)
-        w3_planes = landing("w3_planes", [P, PASSES * K], U8)
+        w2_planes = tile("w2_planes", [P, PASSES * K], U8)
+        w3_planes = tile("w3_planes", [P, PASSES * K], U8)
+        lean_rows = tile("lean_rows", [P, P], F32)
         nc.vector.memset(w3_planes[:].bitcast(I32), 0)
         nc.vector.memset(w2_planes[:].bitcast(I32), 0)
-        tab = [landing("tab%d" % a, [P, T], U32) for a in range(PASSES)]
-        nc.sync.dma_start(idx[:], offs)
-        nc.sync.dma_start(idx2[:], offs2)
+        nc.vector.memset(lean_rows[:], 0.0)
+        ident = kept("ident", [P, P], F32)
+        make_identity(nc, ident[:])
 
-        def load_tab(a):
-            nc.sync.dma_start(tab[a][:].bitcast(I32), tab_words[a].rearrange("p t i -> p (t i)").bitcast(I32))
-
-
-        w3c = {}
-
-        def load_w3(a, alloc):
-            w3c[a] = alloc("w3c%d" % a, [P, K], U32)
-            nc.sync.dma_start(w3c[a][:].bitcast(I32), w3_words[a].rearrange("p c i -> p (c i)").bitcast(I32))
-
+        tab = [tile("tab%d" % a, [P, T], U32) for a in range(PASSES)]
+        w3_codes.append(tile("w3_codes1", [P, K], U32))
+        w2_codes = tile("w2_codes", [P, PASSES * 2 * K], U8)
+        v_planes = tile("v_planes", [P, S], U8)
         w1_raw = {}
 
-        def load_w1(chunk, alloc=landing):
-            a, c0, c1 = chunk
-            w1_raw[chunk] = alloc("w1_raw%d_%d" % (a, c0), [P, PACK, c1 - c0], F32)
-            nc.sync.dma_start(
-                w1_raw[chunk][:], w1[KP * a : KP * (a + 1), c0:c1].rearrange("(p i) r -> p i r", i=PACK)
-            )
+        def load_words(dst, words):
+            nc.sync.dma_start(dst[:].bitcast(I32), words.rearrange("p c i -> p (c i)").bitcast(I32))
 
-        v_words = {(a, h): sb("v_words%d%d" % (a, h), [P, S // 2], U32) for a in range(PASSES) for h in range(2)}
-        v2_words = {}
-        v_planes = sb("v_planes", [P, S], U8)
-        v2_planes = {}
+        def load_weight_planes(queue, planes, scales):
+            for q in range(QUADRANTS):
+                queue.dma_start(
+                    planes[32 * q : 32 * q + ROWS, :].bitcast(I32).rearrange("i (a c) -> i a c", a=PASSES),
+                    scales[:, ROWS * q : ROWS * (q + 1), :].bitcast(I32).rearrange("a i c -> i a c"),
+                )
+
+        def load_w1(chunk):
+            a, c0, c1, share = chunk
+            w1_raw[chunk] = tile("w1_raw%d_%d" % (a, c0), [P, PACK, c1 - c0], F32)
+            rows = w1[PASS * a : PASS * (a + 1), c0:c1]
+            nc.sync.dma_start(w1_raw[chunk][:], rows.rearrange("(p t) r -> p t r", t=PACK))
 
         def gather(dst, window, offsets):
-            nc.vector.tensor_copy(dst[:], window[:].indirect(offsets[:]))
+            nc.vector.tensor_copy(dst[:], window[:].indirect(offsets))
 
-        def gather_v2_planes(half, tag=""):
-            v2_planes[half] = landing("v2_planes%d" % half, [P, S2 // 2], U8, tag)
-            gather(v2_planes[half], tab_planes, idx2[:, 32 * half : 32 * (half + 1)])
-
-        def gather_v2_words(a, m0, m1):
-            piece = landing("v2_words%d_%d" % (a, m0), [P, (m1 - m0) * P], U32)
-            for mt in range(m0, m1):
-                v2_words[a, mt] = piece[:, (mt - m0) * P : (mt - m0 + 1) * P]
-            gather(piece, tab[a], idx2[:, 8 * m0 : 8 * m1])
-
-        def load_planes(queue, planes, scales):
-            for q in range(4):
-                queue.dma_start(
-                    planes[32 * q : 32 * q + 4, :].bitcast(I32).rearrange("r (a c) -> r a c", a=PASSES),
-                    scales[:, 4 * q : 4 * q + 4, :].bitcast(I32).rearrange("a r c -> r a c"),
-                )
-
-        def load_tab_planes():
-            for q in range(4):
-                nc.sync.dma_start(
-                    tab_planes[32 * q : 32 * q + 8, :].bitcast(I32), tab_scales[:, 4 * q : 4 * q + 4, :].bitcast(I32)
-                )
-
-        def shift_plane():
-            gather(v_planes, tab_planes, idx)
-            for q in range(4):
-                nc.sync.dma_start(
-                    v_plane1[32 * q : 32 * q + 4, :].bitcast(I32), v_planes[32 * q + 4 : 32 * q + 8, :].bitcast(I32)
-                )
-
-        w2c = landing("w2c", [P, PASSES * 2 * K], U8)
-
-        def load_w2():
+        load_weight_planes(nc.gpsimd, w2_planes, w2_scales)
+        nc.sync.dma_start(idx[:], offs)
+        nc.sync.dma_start(idx2[:], offs2)
+        load_words(w3_codes[0], w3_words[0])
+        for q in range(QUADRANTS):
             nc.sync.dma_start(
-                w2c[:].bitcast(I32).rearrange("p (a c) -> p a c", a=PASSES),
-                w2_words.bitcast(I32).rearrange("a p c -> p a c"),
+                tab_planes[32 * q : 32 * q + PASSES * ROWS, :].bitcast(I32),
+                tab_scales[:, ROWS * q : ROWS * (q + 1), :].bitcast(I32),
             )
-
-        load_planes(nc.gpsimd, w2_planes, w2_scales)
-        make_identity(nc, ident[:])
-        load_w3(0, sb)
-        load_tab_planes()
-        load_tab(0)
-        load_planes(nc.sync, w3_planes, w3_scales)
+        load_words(tab[0], tab_words[0])
+        load_weight_planes(nc.sync, w3_planes, w3_scales)
         load_w1(W1_CHUNKS[0])
-        load_tab(1)
-        load_w3(1, landing)
-        shift_plane()
-        load_w2()
-        load_w1(W1_CHUNKS[1])
-        load_w1(W1_CHUNKS[2])
-        load_w1(W1_CHUNKS[3])
-        load_w1(W1_CHUNKS[4])
-        lean_col = landing("lean_col", [P, MT], F32)
-        with nc.allow_non_contiguous_dma(reason="one offset for each partition and tile of approved names"):
-            nc.sync.dma_start(lean_col[:], lean.rearrange("(t p) -> p t", p=P))
+        load_words(tab[1], tab_words[1])
+        load_words(w3_codes[1], w3_words[1])
+        gather(v_planes, tab_planes, idx[:])
+        for q in range(QUADRANTS):
+            nc.sync.dma_start(
+                v_plane1[32 * q : 32 * q + ROWS, :].bitcast(I32),
+                v_planes[32 * q + ROWS : 32 * q + 2 * ROWS, :].bitcast(I32),
+            )
+        nc.sync.dma_start(
+            w2_codes[:].bitcast(I32).rearrange("p (a c) -> p a c", a=PASSES),
+            w2_words.bitcast(I32).rearrange("a p c -> p a c"),
+        )
+        for chunk in W1_CHUNKS[1:]:
+            load_w1(chunk)
+        nc.sync.dma_start(lean_rows[0:M_TILES, :], lean.rearrange("(t p) -> t p", p=P))
 
-        for h in range(2):
-            gather(v_words[0, h], tab[0], idx[:, 16 * h : 16 * (h + 1)])
-        gather_v2_planes(0)
-        gather_v2_words(0, 0, 4)
-        for h in range(2):
-            gather(v_words[1, h], tab[1], idx[:, 16 * h : 16 * (h + 1)])
-        gather_v2_words(1, 0, 4)
+        v_words = [tile("v_words%d" % a, [P, S], U32) for a in range(PASSES)]
+        v2_words = [tile("v2_words%d" % a, [P, S2], U32) for a in range(PASSES)]
+        v2_planes = tile("v2_planes", [P, S2], U8)
+        gather(v2_planes, tab_planes, idx2[:])
+        for a in range(PASSES):
+            for half in range(2):
+                offsets = idx[:, half * J_HALF // PER_COLUMN : (half + 1) * J_HALF // PER_COLUMN]
+                gather(v_words[a][:, half * J_HALF : (half + 1) * J_HALF], tab[a], offsets)
+            gather(v2_words[a], tab[a], idx2[:])
 
-        def v_operand(a, jt, at_zero=False):
+        def product_pass(acc, a, jt, codes, plane, start, stop, v_plane_at_row_0=False):
             cols = slice(jt * P, (jt + 1) * P)
-            plane = v_plane1[:, cols] if at_zero and a == 1 else v_planes[4 * a : P, cols]
-            return dict(lhsT=v_words[a, jt // 2][:, jt % 2 * P : (jt % 2 + 1) * P].bitcast(FP8X4), lhsT_scale=plane)
-
-        def w2_pass(acc, rh, a, jt):
+            v_plane = v_plane1[:, cols] if v_plane_at_row_0 and a == 1 else v_planes[ROWS * a : P, cols]
             nc.tensor.matmul_mx(
-                out=acc[:],
-                rhs=w2c[:, 2 * (K * a + HALF * rh) : 2 * (K * a + HALF * (rh + 1))].bitcast(FP4X4),
-                rhs_scale=w2_planes[:, K * a + HALF * rh : K * a + HALF * (rh + 1)],
-                start=(a == 0),
-                stop=(a == PASSES - 1),
-                **v_operand(a, jt, True),
-            )
-
-        def w3_pass(acc, rh, a, jt):
-            nc.tensor.matmul_mx(
-                out=acc[:],
-                rhs=w3c[a][:, HALF * rh : HALF * (rh + 1)].bitcast(FP8X4),
-                rhs_scale=w3_planes[:, K * a + HALF * rh : K * a + HALF * (rh + 1)],
-                start=(a == 0),
-                stop=(a == PASSES - 1),
-                **v_operand(a, jt),
-            )
-
-        w1_grouped = {}
-        w1_codes = {}
-        w1_plane = {}
-
-        def cast_w1(chunk):
-            a, c0, c1 = chunk
-            grouped = landing("w1_grouped%d_%d" % (a, c0), [P, c1 - c0, PACK], BF16)
-            w1_grouped[chunk] = grouped
-            raw = w1_raw[chunk]
-            share = SCALAR_COLS[W1_CHUNKS.index(chunk)]
-            if share:
-                nc.scalar.copy(
-                    grouped[:, :share, :].rearrange("p (c i) t -> p c t i", i=4),
-                    raw[:, :, :share].rearrange("p t (c i) -> p c t i", i=4),
-                )
-            if share < c1 - c0:
-                nc.vector.tensor_copy(
-                    grouped[:, share:, :].rearrange("p (c i) t -> p c t i", i=4),
-                    raw[:, :, share:].rearrange("p t (c i) -> p c t i", i=4),
-                )
-
-        def quantize_w1(chunk):
-            a, c0, c1 = chunk
-            w1_codes[chunk] = landing("w1_codes%d_%d" % (a, c0), [P, c1 - c0], U32)
-            w1_plane[chunk] = landing("w1_plane%d_%d" % (a, c0), [P, c1 - c0], U8)
-            nc.vector.quantize_mx(
-                out=w1_codes[chunk][:].bitcast(FP8X4),
-                scales=w1_plane[chunk][:],
-                in_=w1_grouped[chunk][:].rearrange("p c t -> p (c t)"),
-            )
-
-        def w1_pass(acc, chunk, jt):
-            a, c0, c1 = chunk
-            nc.tensor.matmul_mx(
-                out=acc[:, c0 % HALF : (c1 - 1) % HALF + 1],
-                rhs=w1_codes[chunk][:].bitcast(FP8X4),
-                rhs_scale=w1_plane[chunk][:],
-                start=(a == 0),
-                stop=(a == PASSES - 1 and c1 % HALF == 0),
-                **v_operand(a, jt),
+                out=acc,
+                lhsT=v_words[a][:, cols].bitcast(FP8X4),
+                lhsT_scale=v_plane,
+                rhs=codes,
+                rhs_scale=plane,
+                start=start,
+                stop=stop,
             )
 
         def dealt(acc):
             return acc[:].rearrange("j (p u e) -> j u p e", u=2, e=2)
 
-        def as_dealt(tile):
-            return tile[:].rearrange("j (u p e) -> j u p e", u=2, e=2)
+        def as_dealt(sb):
+            return sb[:].rearrange("j (u p e) -> j u p e", u=2, e=2)
 
-        smaller = {}
-
-        units = [(rh, jt) for jt in range(JT) for rh in range(2)]
-
-        def unit_bank(rh, jt):
-            return bank(JT * rh + jt, [P, HALF])
-
-        end_acc = {unit: unit_bank(*unit) for unit in units}
+        units = [(rh, jt) for jt in range(J_TILES) for rh in range(PASSES)]
+        end_acc = {unit: bank(*unit, [P, PASS]) for unit in units}
+        for a in range(PASSES):
+            for rh, jt in units:
+                r_cols = slice(PASS * rh, PASS * (rh + 1))
+                plane = w3_planes[:, K * a : K * (a + 1)][:, r_cols]
+                product_pass(end_acc[rh, jt][:], a, jt, w3_codes[a][:, r_cols].bitcast(FP8X4), plane, a == 0, a == 1)
         end_sb = {}
-        for jt in range(JT):
-            for rh in range(2):
-                w3_pass(end_acc[rh, jt], rh, 0, jt)
         for rh, jt in units:
-            w3_pass(end_acc[rh, jt], rh, 1, jt)
-        gather_v2_planes(1, "w3c1")
-        gather_v2_words(0, 4, 8)
-        gather_v2_words(1, 4, 8)
-        for rh, jt in units:
-            end_sb[rh, jt] = landing("end_sb%d%d" % (rh, jt), [P, HALF], F32)
+            end_sb[rh, jt] = tile("end_sb%d%d" % (rh, jt), [P, PASS], F32)
             nc.scalar.copy(as_dealt(end_sb[rh, jt]), dealt(end_acc[rh, jt]))
+
         start_acc = {}
-
-        def start_product(rh, jt):
-            start_acc[rh, jt] = unit_bank(rh, jt)
+        for rh, jt in units:
+            start_acc[rh, jt] = bank(rh, jt, [P, PASS])
             for a in range(PASSES):
-                w2_pass(start_acc[rh, jt], rh, a, jt)
+                c0 = K * a + PASS * rh
+                codes = w2_codes[:, 2 * c0 : 2 * (c0 + PASS)].bitcast(FP4X4)
+                product_pass(start_acc[rh, jt][:], a, jt, codes, w2_planes[:, c0 : c0 + PASS], a == 0, a == 1, True)
 
-        def take_min(rh, jt):
-            smaller[rh, jt] = landing("smaller%d%d" % (rh, jt), [P, HALF], F32)
-            nc.vector.tensor_tensor(
-                as_dealt(smaller[rh, jt]), dealt(start_acc[rh, jt]), as_dealt(end_sb[rh, jt]), ALU.min
+        w1_codes = {}
+        w1_plane = {}
+
+        def quantize_w1(chunk):
+            a, c0, c1, share = chunk
+            grouped = tile("w1_grouped%d_%d" % (a, c0), [P, c1 - c0, PACK], BF16)
+            for copy, g0, g1 in ((nc.scalar.copy, 0, share), (nc.vector.tensor_copy, share, c1 - c0)):
+                if g0 < g1:
+                    copy(
+                        grouped[:, g0:g1, :].rearrange("p (c i) t -> p c t i", i=2),
+                        w1_raw[chunk][:, :, g0:g1].rearrange("p t (c i) -> p c t i", i=2),
+                    )
+            w1_codes[chunk] = tile("w1_codes%d_%d" % (a, c0), [P, c1 - c0], U32)
+            w1_plane[chunk] = tile("w1_plane%d_%d" % (a, c0), [P, c1 - c0], U8)
+            nc.vector.quantize_mx(
+                out=w1_codes[chunk][:].bitcast(FP8X4),
+                scales=w1_plane[chunk][:],
+                in_=grouped[:].rearrange("p c t -> p (c t)"),
             )
 
-        h_rows = {}
-
-        def take_max(rh, jt):
-            h_rows[rh, jt] = landing("h_rows%d%d" % (rh, jt), [P, HALF], BF16)
-            nc.vector.tensor_tensor(as_dealt(h_rows[rh, jt]), dealt(look[rh, jt]), as_dealt(smaller[rh, jt]), ALU.max)
-
-        h_grouped = {}
         h_codes = {}
         h_plane = {}
 
-        def turn(rh, piece):
-            turned = bank(JT * rh + piece[0], [P, len(piece), 2, P])
-            for t, jt in enumerate(piece):
-                words = h_rows[rh, jt][:].bitcast(F32)
-                for u in range(2):
-                    nc.tensor.transpose(turned[:, t, u, :], words[:, u * P : (u + 1) * P], ident[:])
-            h_grouped[rh, piece] = landing("h_grouped%d%d" % (rh, piece[0]), [P, len(piece) * P * PACK], BF16)
-            copy_out = nc.vector.tensor_copy if (rh, piece) in LAST_ON_VECTOR else nc.scalar.copy
-            copy_out(
-                h_grouped[rh, piece][:].bitcast(F32).rearrange("p (t j u) -> p t j u", t=len(piece), u=2),
-                turned[:].rearrange("p t u j -> p t j u"),
-            )
-
-        def quantize_h(rh, piece):
-            h_codes[rh, piece] = landing("h_codes%d%d" % (rh, piece[0]), [P, len(piece) * P], U32)
-            h_plane[rh, piece] = landing("h_plane%d%d" % (rh, piece[0]), [P, len(piece) * P], U8)
-            nc.vector.quantize_mx(
-                out=h_codes[rh, piece][:].bitcast(FP8X4), scales=h_plane[rh, piece][:], in_=h_grouped[rh, piece][:]
-            )
-
-        def match_pass(acc, tiles, b, piece):
-            for t, mt in enumerate(tiles):
-                nc.tensor.matmul_mx(
-                    out=acc[:, t, :],
-                    lhsT=v2_words[b, mt].bitcast(FP8X4),
-                    lhsT_scale=v2_planes[mt // 4][4 * b : P, mt % 4 * P : (mt % 4 + 1) * P],
-                    rhs=h_codes[b, piece][:].bitcast(FP8X4),
-                    rhs_scale=h_plane[b, piece][:],
-                    start=(b == 0 and t == 0),
-                    stop=(b == PASSES - 1 and t == len(tiles) - 1),
+        def make_h(jh):
+            tiles = J_HALVES[jh]
+            smaller = {}
+            look = {}
+            for jt in tiles:
+                for rh in range(PASSES):
+                    smaller[rh, jt] = tile("smaller%d%d" % (rh, jt), [P, PASS], F32)
+                    nc.vector.tensor_tensor(
+                        as_dealt(smaller[rh, jt]), dealt(start_acc[rh, jt]), as_dealt(end_sb[rh, jt]), ALU.min
+                    )
+                    look[rh, jt] = bank(rh, jt, [P, PASS])
+            if jh == 0:
+                for chunk in W1_CHUNKS:
+                    quantize_w1(chunk)
+            for chunk in W1_CHUNKS:
+                a, c0, c1, share = chunk
+                rh = c0 // PASS
+                for jt in tiles:
+                    acc = look[rh, jt][:, c0 - PASS * rh : c1 - PASS * rh]
+                    closes = a == PASSES - 1 and c1 == PASS * (rh + 1)
+                    product_pass(acc, a, jt, w1_codes[chunk][:].bitcast(FP8X4), w1_plane[chunk][:], a == 0, closes)
+            grouped = {}
+            for rh in range(PASSES):
+                h_rows = {}
+                for jt in tiles:
+                    h_rows[jt] = tile("h_rows%d%d" % (rh, jt), [P, PASS], BF16)
+                    nc.vector.tensor_tensor(
+                        as_dealt(h_rows[jt]), dealt(look[rh, jt]), as_dealt(smaller[rh, jt]), ALU.max
+                    )
+                turned = bank(rh, tiles[0], [P, len(tiles), 2, P])
+                for n, jt in enumerate(tiles):
+                    words = h_rows[jt][:].bitcast(F32)
+                    for u in range(2):
+                        nc.tensor.transpose(turned[:, n, u, :], words[:, u * P : (u + 1) * P], ident[:])
+                grouped[rh] = tile("h_grouped%d%d" % (rh, jh), [P, J_HALF * PACK], BF16)
+                last = jh == len(J_HALVES) - 1 and rh == PASSES - 1
+                copy = nc.vector.tensor_copy if last else nc.scalar.copy
+                copy(
+                    grouped[rh][:].bitcast(F32).rearrange("p (n j u) -> p n j u", n=len(tiles), u=2),
+                    turned[:].rearrange("p n u j -> p n j u"),
+                )
+            for rh in range(PASSES):
+                h_codes[rh, jh] = tile("h_codes%d%d" % (rh, jh), [P, J_HALF], U32)
+                h_plane[rh, jh] = tile("h_plane%d%d" % (rh, jh), [P, J_HALF], U8)
+                nc.vector.quantize_mx(
+                    out=h_codes[rh, jh][:].bitcast(FP8X4), scales=h_plane[rh, jh][:], in_=grouped[rh][:]
                 )
 
-        def finish(acc, tiles, piece):
-            res = landing("res%d%d" % (tiles[0], piece[0]), [P, len(tiles), len(piece) * P], F32)
-            for t, mt in enumerate(tiles):
-                nc.scalar.activation(res[:, t, :], acc[:, t, :], GELU, bias=lean_col[:, mt : mt + 1])
-            nc.sync.dma_start(
-                out[tiles[0] * P : (tiles[-1] + 1) * P, piece[0] * P : (piece[-1] + 1) * P].rearrange(
-                    "(t p) j -> p t j", p=P
-                ),
-                res[:],
-            )
+        def match(jh):
+            tiles = J_HALVES[jh]
+            accs = [bank(rh, jt, [P, 2, J_HALF]) for jt in reversed(tiles) for rh in range(PASSES)]
 
-        def look_passes(chunks, tiles):
-            for chunk in chunks:
-                for jt in tiles:
-                    w1_pass(look[chunk[1] // HALF, jt], chunk, jt)
+            def match_pass(pair, rh):
+                for n in range(2):
+                    cols = slice((2 * pair + n) * P, (2 * pair + n + 1) * P)
+                    nc.tensor.matmul_mx(
+                        out=accs[pair][:, n, :],
+                        lhsT=v2_words[rh][:, cols].bitcast(FP8X4),
+                        lhsT_scale=v2_planes[ROWS * rh : P, cols],
+                        rhs=h_codes[rh, jh][:].bitcast(FP8X4),
+                        rhs_scale=h_plane[rh, jh][:],
+                        start=(rh == 0 and n == 0),
+                        stop=(rh == PASSES - 1 and n == 1),
+                    )
 
-        def open_match(piece, banks, m0=0):
-            per_bank = JT // len(piece)
-            return [(bank(n, [P, per_bank, len(piece) * P]), tuple(range(m0 + i * per_bank, m0 + (i + 1) * per_bank))) for i, n in enumerate(banks)]
+            for pair in range(M_TILES // 2):
+                match_pass(pair, 0)
+            for pair in range(M_TILES // 2):
+                match_pass(pair, 1)
+                result = tile("result%d%d" % (pair, jh), [P, 2, J_HALF], F32)
+                for n in range(2):
+                    mt = 2 * pair + n
+                    nc.scalar.activation(result[:, n, :], accs[pair][:, n, :], GELU, bias=lean_col[:, mt : mt + 1])
+                rows = out[2 * pair * P : 2 * (pair + 1) * P, jh * J_HALF : (jh + 1) * J_HALF]
+                nc.sync.dma_start(rows.rearrange("(n p) j -> p n j", p=P), result[:])
 
-        look = {}
-        for rh, jt in units:
-            start_product(rh, jt)
-        for n, piece in enumerate(PIECES):
-            for jt in piece:
-                for rh in range(2):
-                    take_min(rh, jt)
-                    look[rh, jt] = unit_bank(rh, jt)
-            if n == 0:
-                for chunk in W1_CHUNKS:
-                    cast_w1(chunk)
-                    quantize_w1(chunk)
-            look_passes(W1_CHUNKS, piece)
-            for rh in range(2):
-                for jt in piece:
-                    take_max(rh, jt)
-                turn(rh, piece)
-            for rh in range(2):
-                quantize_h(rh, piece)
-        for piece in PIECES:
-            match = open_match(piece, [JT * rh + jt for jt in reversed(piece) for rh in range(2)])
-            for acc, tiles in match:
-                match_pass(acc, tiles, 0, piece)
-            for acc, tiles in match:
-                match_pass(acc, tiles, 1, piece)
-                finish(acc, tiles, piece)
+        for jh in range(len(J_HALVES)):
+            make_h(jh)
+        lean_turned = bank(0, J_HALVES[0][-1], [P, P])
+        nc.tensor.transpose(lean_turned[:], lean_rows[:], ident[:])
+        lean_col = tile("lean_col", [P, M_TILES], F32)
+        nc.scalar.copy(lean_col[:], lean_turned[:, 0:M_TILES])
+        for jh in range(len(J_HALVES)):
+            match(jh)

@@ -29,7 +29,8 @@ J_HALVES = ((0, 1), (2, 3))
 J_HALF = 2 * P
 M_TILES = S2 // P
 
-W1_CHUNKS = ((0, 0, 512, 512), (1, 0, 512, 512), (0, 512, 1024, 448), (1, 512, 768, 128), (1, 768, 1024, 128))
+W1_CHUNKS = ((0, 0, 512, 512), (1, 0, 512, 256), (0, 512, 1024, 320), (1, 512, 768, 144), (1, 768, 1024, 144))
+GPSIMD_COLUMNS = 128
 
 
 def tile_list_lookalike_name_screening_kernel(
@@ -57,10 +58,6 @@ def tile_list_lookalike_name_screening_kernel(
             zeros = early.tile([P, S // 4], I32, name="zeros")
             nc.gpsimd.memset(zeros[:], 0)
             nc.vector.tensor_copy(v_plane1[:].bitcast(I32), zeros[:])
-        warm = kept("warm", [P, 1], F32)
-        warm_out = kept("warm_out", [P, 1], F32)
-        nc.gpsimd.memset(warm[:], 0.0)
-        nc.scalar.activation(warm_out[:], warm[:], GELU)
         late = ctx.enter_context(tc.tile_pool(name="late", bufs=1))
 
         def tile(name, shape, dtype):
@@ -183,12 +180,16 @@ def tile_list_lookalike_name_screening_kernel(
         def quantize_w1(chunk):
             a, c0, c1, share = chunk
             grouped = tile("w1_grouped%d_%d" % (a, c0), [P, c1 - c0, PACK], BF16)
-            for copy, g0, g1 in ((nc.scalar.copy, 0, share), (nc.vector.tensor_copy, share, c1 - c0)):
-                if g0 < g1:
-                    copy(
-                        grouped[:, g0:g1, :].rearrange("p (c i) t -> p c t i", i=2),
-                        w1_raw[chunk][:, :, g0:g1].rearrange("p t (c i) -> p c t i", i=2),
-                    )
+            raw = w1_raw[chunk]
+            nc.scalar.copy(
+                grouped[:, :share, :].rearrange("p (c i) t -> p c t i", i=2),
+                raw[:, :, :share].rearrange("p t (c i) -> p c t i", i=2),
+            )
+            for g0 in range(share, c1 - c0, GPSIMD_COLUMNS):
+                g1 = min(g0 + GPSIMD_COLUMNS, c1 - c0)
+                nc.gpsimd.tensor_scalar(
+                    grouped[:, g0:g1, :], raw[:, :, g0:g1].rearrange("p t c -> p c t"), 1.0, 0.0, ALU.mult, ALU.add
+                )
             w1_codes[chunk] = tile("w1_codes%d_%d" % (a, c0), [P, c1 - c0], U32)
             w1_plane[chunk] = tile("w1_plane%d_%d" % (a, c0), [P, c1 - c0], U8)
             nc.vector.quantize_mx(

@@ -198,6 +198,13 @@ def tile_list_lookalike_name_screening_kernel(
                 in_=grouped[:].rearrange("p c t -> p (c t)"),
             )
 
+        lean_col = tile("lean_col", [P, M_TILES], F32)
+
+        def turn_lean():
+            lean_turned = bank(0, J_HALVES[0][-1], [P, P])
+            nc.tensor.transpose(lean_turned[:], lean_rows[:], ident[:])
+            nc.scalar.copy(lean_col[:], lean_turned[:, 0:M_TILES])
+
         h_codes = {}
         h_plane = {}
 
@@ -224,17 +231,18 @@ def tile_list_lookalike_name_screening_kernel(
                     product_pass(acc, a, jt, w1_codes[chunk][:].bitcast(FP8X4), w1_plane[chunk][:], a == 0, closes)
             grouped = {}
             for rh in range(PASSES):
-                h_rows = {}
-                for jt in tiles:
-                    h_rows[jt] = tile("h_rows%d%d" % (rh, jt), [P, PASS], BF16)
+                h_rows = tile("h_rows%d%d" % (rh, jh), [P, len(tiles), PASS], BF16)
+                for n, jt in enumerate(tiles):
                     nc.vector.tensor_tensor(
-                        as_dealt(h_rows[jt]), dealt(look[rh, jt]), as_dealt(smaller[rh, jt]), ALU.max
+                        as_dealt(h_rows[:, n, :]), dealt(look[rh, jt]), as_dealt(smaller[rh, jt]), ALU.max
                     )
                 turned = bank(rh, tiles[0], [P, len(tiles), 2, P])
-                for n, jt in enumerate(tiles):
-                    words = h_rows[jt][:].bitcast(F32)
+                words = h_rows[:].bitcast(F32)
+                for n in reversed(range(len(tiles))):
                     for u in range(2):
-                        nc.tensor.transpose(turned[:, n, u, :], words[:, u * P : (u + 1) * P], ident[:])
+                        nc.tensor.transpose(turned[:, n, u, :], words[:, n, u * P : (u + 1) * P], ident[:])
+                if (jh, rh) == (0, 0):
+                    turn_lean()
                 grouped[rh] = tile("h_grouped%d%d" % (rh, jh), [P, J_HALF * PACK], BF16)
                 last = jh == len(J_HALVES) - 1 and rh == PASSES - 1
                 copy = nc.vector.tensor_copy if last else nc.scalar.copy
@@ -267,9 +275,8 @@ def tile_list_lookalike_name_screening_kernel(
                     )
 
             for pair in range(M_TILES // 2):
-                match_pass(pair, 0)
-            for pair in range(M_TILES // 2):
-                match_pass(pair, 1)
+                for rh in range(PASSES):
+                    match_pass(pair, rh)
                 result = tile("result%d%d" % (pair, jh), [P, 2, J_HALF], F32)
                 for n in range(2):
                     mt = 2 * pair + n
@@ -279,9 +286,5 @@ def tile_list_lookalike_name_screening_kernel(
 
         for jh in range(len(J_HALVES)):
             make_h(jh)
-        lean_turned = bank(0, J_HALVES[0][-1], [P, P])
-        nc.tensor.transpose(lean_turned[:], lean_rows[:], ident[:])
-        lean_col = tile("lean_col", [P, M_TILES], F32)
-        nc.scalar.copy(lean_col[:], lean_turned[:, 0:M_TILES])
         for jh in range(len(J_HALVES)):
             match(jh)

from contextlib import ExitStack

import concourse.mybir as mybir
from concourse.masks import make_identity

K, T, S, S2 = 1024, 2048, 512, 1024
FLOPS = 2 * K * K * S * 3 + 2 * K * S2 * S

F32 = mybir.dt.float32
BF16 = mybir.dt.bfloat16
I32 = mybir.dt.int32
U32 = mybir.dt.uint32
U16 = mybir.dt.uint16
U8 = mybir.dt.uint8
FP8X4 = mybir.dt.float8_e4m3fn_x4
FP4X4 = mybir.dt.float4_e2m1fn_x4
ALU = mybir.AluOpType
GELU = mybir.ActivationFunctionType.Gelu_apprx_tanh

P = 128
PACK = 4
PASS = P * PACK
PASSES = K // PASS
QUADRANTS = 4
ROWS = 4
PER_COLUMN = 16
J_TILES = S // P
J_HALVES = ((0, 1), (2, 3))
J_HALF = 2 * P
M_TILES = S2 // P

W1_CHUNKS = ((0, 0, 512, 512), (1, 0, 512, 256), (0, 512, 1024, 320), (1, 512, 768, 144), (1, 768, 1024, 144))
GPSIMD_COLUMNS = 128


def tile_list_lookalike_name_screening_kernel(
    tc, tab_words, tab_scales, offs, offs2, w1, w2_words, w2_scales, w3_words, w3_scales, lean, out
):
    nc = tc.nc
    with ExitStack() as ctx:
        keep = ctx.enter_context(tc.tile_pool(name="keep", bufs=1))
        psum = ctx.enter_context(tc.psum_pool(name="psum", bufs=1))

        def kept(name, shape, dtype):
            return keep.tile(shape, dtype, name=name, align_bytes=64)

        def bank(rh, jt, shape):
            return psum.tile(shape, F32, name="bank%d%d" % (rh, jt))

        idx = kept("idx", [P, S // PER_COLUMN], U16)
        idx2 = kept("idx2", [P, S2 // PER_COLUMN], U16)
        tab_planes = kept("tab_planes", [P, T], U8)
        v_plane1 = kept("v_plane1", [P, S], U8)
        w3_codes = [kept("w3_codes0", [P, K], U32)]

        nc.vector.memset(tab_planes[:].bitcast(I32), 0)
        with tc.tile_pool(name="early", bufs=1) as early:
            zeros = early.tile([P, S // 4], I32, name="zeros")
            nc.gpsimd.memset(zeros[:], 0)
            nc.vector.tensor_copy(v_plane1[:].bitcast(I32), zeros[:])
        late = ctx.enter_context(tc.tile_pool(name="late", bufs=1))

        def tile(name, shape, dtype):
            return late.tile(shape, dtype, name=name, align_bytes=64)

        w2_planes = tile("w2_planes", [P, PASSES * K], U8)
        w3_planes = tile("w3_planes", [P, PASSES * K], U8)
        lean_rows = tile("lean_rows", [P, P], F32)
        nc.vector.memset(w3_planes[:].bitcast(I32), 0)
        nc.vector.memset(w2_planes[:].bitcast(I32), 0)
        nc.vector.memset(lean_rows[:], 0.0)
        ident = kept("ident", [P, P], F32)
        make_identity(nc, ident[:])

        tab = [tile("tab%d" % a, [P, T], U32) for a in range(PASSES)]
        w3_codes.append(tile("w3_codes1", [P, K], U32))
        w2_codes = tile("w2_codes", [P, PASSES * 2 * K], U8)
        v_planes = tile("v_planes", [P, S], U8)
        w1_raw = {}

        def load_words(dst, words):
            nc.sync.dma_start(dst[:].bitcast(I32), words.rearrange("p c i -> p (c i)").bitcast(I32))

        def load_weight_planes(queue, planes, scales):
            for q in range(QUADRANTS):
                queue.dma_start(
                    planes[32 * q : 32 * q + ROWS, :].bitcast(I32).rearrange("i (a c) -> i a c", a=PASSES),
                    scales[:, ROWS * q : ROWS * (q + 1), :].bitcast(I32).rearrange("a i c -> i a c"),
                )

        def load_w1(chunk):
            a, c0, c1, share = chunk
            w1_raw[chunk] = tile("w1_raw%d_%d" % (a, c0), [P, PACK, c1 - c0], F32)
            rows = w1[PASS * a : PASS * (a + 1), c0:c1]
            nc.sync.dma_start(w1_raw[chunk][:], rows.rearrange("(p t) r -> p t r", t=PACK))

        def gather(dst, window, offsets):
            nc.vector.tensor_copy(dst[:], window[:].indirect(offsets))

        load_weight_planes(nc.gpsimd, w2_planes, w2_scales)
        nc.sync.dma_start(idx[:], offs)
        nc.sync.dma_start(idx2[:], offs2)
        load_words(w3_codes[0], w3_words[0])
        for q in range(QUADRANTS):
            nc.sync.dma_start(
                tab_planes[32 * q : 32 * q + PASSES * ROWS, :].bitcast(I32),
                tab_scales[:, ROWS * q : ROWS * (q + 1), :].bitcast(I32),
            )
        load_words(tab[0], tab_words[0])
        load_weight_planes(nc.sync, w3_planes, w3_scales)
        load_w1(W1_CHUNKS[0])
        load_words(tab[1], tab_words[1])
        load_words(w3_codes[1], w3_words[1])
        gather(v_planes, tab_planes, idx[:])
        for q in range(QUADRANTS):
            nc.sync.dma_start(
                v_plane1[32 * q : 32 * q + ROWS, :].bitcast(I32),
                v_planes[32 * q + ROWS : 32 * q + 2 * ROWS, :].bitcast(I32),
            )
        nc.sync.dma_start(
            w2_codes[:].bitcast(I32).rearrange("p (a c) -> p a c", a=PASSES),
            w2_words.bitcast(I32).rearrange("a p c -> p a c"),
        )
        for chunk in W1_CHUNKS[1:]:
            load_w1(chunk)
        nc.sync.dma_start(lean_rows[0:M_TILES, :], lean.rearrange("(t p) -> t p", p=P))

        v_words = [tile("v_words%d" % a, [P, S], U32) for a in range(PASSES)]
        v2_words = [tile("v2_words%d" % a, [P, S2], U32) for a in range(PASSES)]
        v2_planes = tile("v2_planes", [P, S2], U8)
        gather(v2_planes, tab_planes, idx2[:])
        for a in range(PASSES):
            for half in range(2):
                offsets = idx[:, half * J_HALF // PER_COLUMN : (half + 1) * J_HALF // PER_COLUMN]
                gather(v_words[a][:, half * J_HALF : (half + 1) * J_HALF], tab[a], offsets)
            gather(v2_words[a], tab[a], idx2[:])

        def product_pass(acc, a, jt, codes, plane, start, stop, v_plane_at_row_0=False):
            cols = slice(jt * P, (jt + 1) * P)
            v_plane = v_plane1[:, cols] if v_plane_at_row_0 and a == 1 else v_planes[ROWS * a : P, cols]
            nc.tensor.matmul_mx(
                out=acc,
                lhsT=v_words[a][:, cols].bitcast(FP8X4),
                lhsT_scale=v_plane,
                rhs=codes,
                rhs_scale=plane,
                start=start,
                stop=stop,
            )

        def dealt(acc):
            return acc[:].rearrange("j (p u e) -> j u p e", u=2, e=2)

        def as_dealt(sb):
            return sb[:].rearrange("j (u p e) -> j u p e", u=2, e=2)

        units = [(rh, jt) for jt in range(J_TILES) for rh in range(PASSES)]
        end_acc = {unit: bank(*unit, [P, PASS]) for unit in units}
        for a in range(PASSES):
            for rh, jt in units:
                r_cols = slice(PASS * rh, PASS * (rh + 1))
                plane = w3_planes[:, K * a : K * (a + 1)][:, r_cols]
                product_pass(end_acc[rh, jt][:], a, jt, w3_codes[a][:, r_cols].bitcast(FP8X4), plane, a == 0, a == 1)
        end_sb = {}
        for rh, jt in units:
            end_sb[rh, jt] = tile("end_sb%d%d" % (rh, jt), [P, PASS], F32)
            nc.scalar.copy(as_dealt(end_sb[rh, jt]), dealt(end_acc[rh, jt]))

        start_acc = {}
        for rh, jt in units:
            start_acc[rh, jt] = bank(rh, jt, [P, PASS])
            for a in range(PASSES):
                c0 = K * a + PASS * rh
                codes = w2_codes[:, 2 * c0 : 2 * (c0 + PASS)].bitcast(FP4X4)
                product_pass(start_acc[rh, jt][:], a, jt, codes, w2_planes[:, c0 : c0 + PASS], a == 0, a == 1, True)

        w1_codes = {}
        w1_plane = {}

        def quantize_w1(chunk):
            a, c0, c1, share = chunk
            grouped = tile("w1_grouped%d_%d" % (a, c0), [P, c1 - c0, PACK], BF16)
            raw = w1_raw[chunk]
            nc.scalar.copy(
                grouped[:, :share, :].rearrange("p (c i) t -> p c t i", i=2),
                raw[:, :, :share].rearrange("p t (c i) -> p c t i", i=2),
            )
            for g0 in range(share, c1 - c0, GPSIMD_COLUMNS):
                g1 = min(g0 + GPSIMD_COLUMNS, c1 - c0)
                nc.gpsimd.tensor_scalar(
                    grouped[:, g0:g1, :], raw[:, :, g0:g1].rearrange("p t c -> p c t"), 1.0, 0.0, ALU.mult, ALU.add
                )
            w1_codes[chunk] = tile("w1_codes%d_%d" % (a, c0), [P, c1 - c0], U32)
            w1_plane[chunk] = tile("w1_plane%d_%d" % (a, c0), [P, c1 - c0], U8)
            nc.vector.quantize_mx(
                out=w1_codes[chunk][:].bitcast(FP8X4),
                scales=w1_plane[chunk][:],
                in_=grouped[:].rearrange("p c t -> p (c t)"),
            )

        lean_col = tile("lean_col", [P, M_TILES], F32)

        def turn_lean():
            lean_turned = bank(0, J_HALVES[0][-1], [P, P])
            nc.tensor.transpose(lean_turned[:], lean_rows[:], ident[:])
            nc.scalar.copy(lean_col[:], lean_turned[:, 0:M_TILES])

        h_codes = {}
        h_plane = {}

        def make_h(jh):
            tiles = J_HALVES[jh]
            smaller = {}
            look = {}
            for jt in tiles:
                for rh in range(PASSES):
                    smaller[rh, jt] = tile("smaller%d%d" % (rh, jt), [P, PASS], F32)
                    nc.vector.tensor_tensor(
                        as_dealt(smaller[rh, jt]), dealt(start_acc[rh, jt]), as_dealt(end_sb[rh, jt]), ALU.min
                    )
                    look[rh, jt] = bank(rh, jt, [P, PASS])
            if jh == 0:
                for chunk in W1_CHUNKS:
                    quantize_w1(chunk)
            for chunk in W1_CHUNKS:
                a, c0, c1, share = chunk
                rh = c0 // PASS
                for jt in tiles:
                    acc = look[rh, jt][:, c0 - PASS * rh : c1 - PASS * rh]
                    closes = a == PASSES - 1 and c1 == PASS * (rh + 1)
                    product_pass(acc, a, jt, w1_codes[chunk][:].bitcast(FP8X4), w1_plane[chunk][:], a == 0, closes)
            grouped = {}
            for rh in range(PASSES):
                h_rows = tile("h_rows%d%d" % (rh, jh), [P, len(tiles), PASS], BF16)
                for n, jt in enumerate(tiles):
                    nc.vector.tensor_tensor(
                        as_dealt(h_rows[:, n, :]), dealt(look[rh, jt]), as_dealt(smaller[rh, jt]), ALU.max
                    )
                turned = bank(rh, tiles[0], [P, len(tiles), 2, P])
                words = h_rows[:].bitcast(F32)
                for n in reversed(range(len(tiles))):
                    for u in range(2):
                        nc.tensor.transpose(turned[:, n, u, :], words[:, n, u * P : (u + 1) * P], ident[:])
                if (jh, rh) == (0, 0):
                    turn_lean()
                grouped[rh] = tile("h_grouped%d%d" % (rh, jh), [P, J_HALF * PACK], BF16)
                last = jh == len(J_HALVES) - 1 and rh == PASSES - 1
                copy = nc.vector.tensor_copy if last else nc.scalar.copy
                copy(
                    grouped[rh][:].bitcast(F32).rearrange("p (n j u) -> p n j u", n=len(tiles), u=2),
                    turned[:].rearrange("p n u j -> p n j u"),
                )
            for rh in range(PASSES):
                h_codes[rh, jh] = tile("h_codes%d%d" % (rh, jh), [P, J_HALF], U32)
                h_plane[rh, jh] = tile("h_plane%d%d" % (rh, jh), [P, J_HALF], U8)
                nc.vector.quantize_mx(
                    out=h_codes[rh, jh][:].bitcast(FP8X4), scales=h_plane[rh, jh][:], in_=grouped[rh][:]
                )

        def match(jh):
            tiles = J_HALVES[jh]
            accs = [bank(rh, jt, [P, 2, J_HALF]) for jt in reversed(tiles) for rh in range(PASSES)]

            def match_pass(pair, rh):
                for n in range(2):
                    cols = slice((2 * pair + n) * P, (2 * pair + n + 1) * P)
                    nc.tensor.matmul_mx(
                        out=accs[pair][:, n, :],
                        lhsT=v2_words[rh][:, cols].bitcast(FP8X4),
                        lhsT_scale=v2_planes[ROWS * rh : P, cols],
                        rhs=h_codes[rh, jh][:].bitcast(FP8X4),
                        rhs_scale=h_plane[rh, jh][:],
                        start=(rh == 0 and n == 0),
                        stop=(rh == PASSES - 1 and n == 1),
                    )

            for pair in range(M_TILES // 2):
                for rh in range(PASSES):
                    match_pass(pair, rh)
                result = tile("result%d%d" % (pair, jh), [P, 2, J_HALF], F32)
                for n in range(2):
                    mt = 2 * pair + n
                    nc.scalar.activation(result[:, n, :], accs[pair][:, n, :], GELU, bias=lean_col[:, mt : mt + 1])
                rows = out[2 * pair * P : 2 * (pair + 1) * P, jh * J_HALF : (jh + 1) * J_HALF]
                nc.sync.dma_start(rows.rearrange("(n p) j -> p n j", p=P), result[:])

        for jh in range(len(J_HALVES)):
            make_h(jh)
        for jh in range(len(J_HALVES)):
            match(jh)
